import numpy as np
import ml_dtypes


def mxq(x, axis, fmt="e4m3"):
    dtype, down = {"e4m3": (ml_dtypes.float8_e4m3fn, 7), "e5m2": (ml_dtypes.float8_e5m2, 14)}[fmt]
    v = np.moveaxis(np.asarray(x, np.float32).astype(ml_dtypes.bfloat16).astype(np.float64), axis, -1)
    blocks = v.reshape(v.shape[:-1] + (-1, 32))
    amax = np.abs(blocks).max(-1, keepdims=True)
    byte = np.maximum(np.where(amax > 0, np.frexp(amax)[1] - 1 + 127, 0) - down, 1)
    scale = np.exp2(byte - 127.0)
    codes = (blocks / scale).astype(np.float32).astype(dtype).astype(np.float64)
    return np.moveaxis((codes * scale).reshape(v.shape), -1, axis)


WIDE = False


def mx_kscale(k):
    if not WIDE:
        return np.ones(k)
    levels = np.array([10, -10, 5, -5, 0])
    if k % 512:
        return np.exp2(np.random.permutation(np.resize(levels, k // 32))).repeat(32)
    a = np.empty((k // 512, 16))
    for p in range(k // 512):
        a[p, :8] = np.random.permutation(np.resize(levels, 8))
        for g in range(8):
            far = levels[np.abs(levels - a[p, g]) >= 10]
            a[p, g + 8] = far[np.random.randint(len(far))]
    return np.exp2(a.ravel()).repeat(32)


def f64(x):
    return np.asarray(x).astype(np.float64)


def striped(idx):
    return np.tile(idx.reshape(-1, 16).T, (8, 1)).astype(np.uint16)


def unstriped(offs):
    return offs[:16].T.reshape(-1).astype(np.int64)


def striped8(idx):
    return np.concatenate([x.reshape(-1, 16).T for x in idx]).astype(np.uint16)


def runs(offs, k):
    lists = np.stack([offs[16 * r : 16 * r + 16].T.reshape(-1) for r in range(8)]).astype(np.int64)
    return lists[np.arange(k) % 512 // 64]


def pack_weight(w):
    k, n = w.shape
    w = f64(np.asarray(w, np.float32).astype(ml_dtypes.bfloat16)).reshape(k // 32, 32, n)
    amax = np.abs(w).max(1)
    byte = np.clip(np.where(amax > 0, np.frexp(amax)[1] - 1 + 127 - 7, 1), 1, 254)
    scaled = (w * np.exp2(127.0 - byte)[:, None, :]).reshape(k, n).astype(np.float32)
    words = np.ascontiguousarray(scaled.reshape(k // 512, 128, 4, n).transpose(0, 1, 3, 2)).astype(ml_dtypes.float8_e4m3fn).view(np.uint8)
    return words, np.ascontiguousarray(byte.astype(np.uint8).reshape(k // 512, 16, n))


def unpack_weight(words, scales):
    g, p, n, _ = words.shape
    vals = np.ascontiguousarray(words).view(ml_dtypes.float8_e4m3fn).astype(np.float64) * np.repeat(np.exp2(scales.astype(np.float64) - 127.0), 8, axis=1)[..., None]
    return vals.transpose(0, 1, 3, 2).reshape(g * 512, n)


K, T, S, V, H = 512, 2048, 512, 512, 512


def setup_inputs():
    n = np.random.standard_normal
    s = mx_kscale(K)[:, None]
    u = mx_kscale(S)
    packed_xT = pack_weight(n((K, T)) * s)
    return {
        "x_words": packed_xT[0],
        "x_scales": packed_xT[1],
        "w1": (n((K, H)) / np.sqrt(K) / s).astype(np.float32),
        "w2": (n((K, H)) / np.sqrt(K) / s).astype(np.float32),
        "w3": (n((K, H)) / np.sqrt(K) / s).astype(np.float32),
        "ga": (np.random.uniform(0.5, 1.5, (H, 1)) * u[:, None]).astype(np.float32),
        "gb": (np.random.uniform(0.5, 1.5, (H, 1)) / u[:, None]).astype(np.float32),
        "offs": striped(np.random.permutation(T)[:S]),
        "two": striped(np.random.permutation(T)[:S]),
        "n1": striped8(np.stack([np.random.permutation(S) for _ in range(8)])),
        "n2": striped8(np.stack([np.random.permutation(S) for _ in range(8)])),
        "three": striped(np.random.permutation(T)[:V]),
        "n3": striped8(np.stack([np.random.permutation(V) for _ in range(8)])),
        "n4": striped8(np.stack([np.random.permutation(V) for _ in range(8)])),
        "n5": striped8(np.stack([np.random.permutation(V) for _ in range(8)])),
        "n6": striped8(np.stack([np.random.permutation(V) for _ in range(8)])),
    }


def reference(x_words, x_scales, w1, w2, w3, ga, gb, offs, two, n1, n2, three, n3, n4, n5, n6):
    xq = unpack_weight(x_words, x_scales)[:, unstriped(offs)]
    y = mxq(f64(w1), 0, "e4m3").T @ xq
    x_two = unpack_weight(x_words, x_scales)[:, unstriped(two)]
    d = mxq(f64(w2), 0, "e4m3").T @ x_two
    z = f64(ga) * (0.75 * (y * (d[np.arange(H)[:, None], runs(n2, H)]) - ((y[np.arange(H)[:, None], runs(n1, H)]) * d)))
    x_three = unpack_weight(x_words, x_scales)[:, unstriped(three)]
    b = mxq(f64(w3), 0, "e4m3").T @ x_three
    pa = b[np.arange(H)[:, None], runs(n3, H)]
    pb = b[np.arange(H)[:, None], runs(n4, H)]
    z2 = f64(gb) * (np.maximum(np.minimum(b, pa), np.minimum(np.maximum(b, pa), pb)))
    s = 0.0625 * ((mxq(z, 0, "e4m3").T @ mxq(z2, 0, "e4m3")))
    return np.minimum(np.maximum(s, s[np.arange(S)[:, None], runs(n5, S)]), s[np.arange(S)[:, None], runs(n6, S)])

@@ -1,0 +1,310 @@
+from contextlib import ExitStack
+
+import concourse.mybir as mybir
+from concourse.masks import make_identity
+
+K, T, S, V, H = 512, 2048, 512, 512, 512
+FLOPS = 4 * 2 * 512 * 512 * 512
+
+F32 = mybir.dt.float32
+BF16 = mybir.dt.bfloat16
+I32 = mybir.dt.int32
+U32 = mybir.dt.uint32
+U16 = mybir.dt.uint16
+U8 = mybir.dt.uint8
+FP8X4 = mybir.dt.float8_e4m3fn_x4
+ALU = mybir.AluOpType
+ACT = mybir.ActivationFunctionType
+
+P = 128
+N = 512
+HALF = 256
+WIDE = 1024
+
+
+def tile_picked_twkcrossbmedminmx_none_p_kernel(
+    tc, x_words, x_scales, w1, w2, w3, ga, gb, offs, two, n1, n2, three, n3, n4, n5, n6, out
+):
+    nc = tc.nc
+    with ExitStack() as ctx:
+        lists = ctx.enter_context(tc.tile_pool(name="lists", bufs=1))
+        keep = ctx.enter_context(tc.tile_pool(name="keep", bufs=1))
+        ps_mm = ctx.enter_context(tc.psum_pool(name="ps_mm", bufs=3))
+        ps_sum = ctx.enter_context(tc.psum_pool(name="ps_sum", bufs=2))
+        ps_back = ctx.enter_context(tc.psum_pool(name="ps_back", bufs=3))
+
+        def sb(name, shape, dtype):
+            return keep.tile(shape, dtype, name=name, align_bytes=64)
+
+        def load_list(name, src):
+            tile = lists.tile([P, N // 16], U16, name=name)
+            nc.sync.dma_start(tile[:], src)
+            return tile
+
+        xs = sb("xs", [P, T], U8)
+        nc.gpsimd.memset(xs[:].bitcast(I32), 0)
+        l_three = load_list("l_three", three)
+        l_offs = load_list("l_offs", offs)
+        l_two = load_list("l_two", two)
+        for q in range(4):
+            nc.sync.dma_start(xs[32 * q : 32 * q + 4, :].bitcast(I32), x_scales[0, 4 * q : 4 * q + 4, :].bitcast(I32))
+
+        def load_w(name, w, c0, c1):
+            raw = sb(name, [P, 4, c1 - c0], F32)
+            nc.sync.dma_start(raw[:], w.rearrange("(p j) c -> p j c", j=4)[:, :, c0:c1])
+            return raw
+
+        w3_raw = load_w("w3_raw", w3, 0, N)
+        g_rows = sb("g_rows", [P, P], F32)
+        nc.gpsimd.memset(g_rows[:], 0.0)
+        for a, g in enumerate((ga, gb)):
+            nc.sync.dma_start(
+                g_rows[4 * a : 4 * a + 4, :].rearrange("t (b r) -> t b r", r=8),
+                g.rearrange("(b t r) o -> t b (r o)", t=4, r=8),
+            )
+        xw = sb("xw", [P, T], U32)
+        nc.sync.dma_start(xw[:].bitcast(I32), x_words[0].rearrange("p n t -> p (n t)").bitcast(I32))
+        l_n3 = load_list("l_n3", n3)
+        l_n4 = load_list("l_n4", n4)
+        w1_raw = load_w("w1_raw", w1, 0, N)
+        w2_raw = load_w("w2_raw", w2, 0, N)
+        l_n2 = load_list("l_n2", n2)
+        l_n1 = load_list("l_n1", n1)
+        l_n5 = load_list("l_n5", n5)
+        l_n6 = load_list("l_n6", n6)
+
+        ident = sb("ident", [P, P], F32)
+        make_identity(nc, ident[:])
+
+        b_win = [sb("b_win%d" % t, [P, WIDE if t < 2 else N], F32) for t in range(4)]
+        d_win = [sb("d_win%d" % t, [P, WIDE], F32) for t in range(4)]
+        y_win = [sb("y_win%d" % t, [P, WIDE], F32) for t in range(4)]
+        for tile in b_win[:2]:
+            nc.vector.memset(tile[:, N:WIDE], 0.0)
+
+        def pick(name, src, lst, dtype):
+            got = sb(name, [P, N], dtype)
+            nc.vector.tensor_copy(got[:], src[:].indirect(lst[:]))
+            return got
+
+        xs3 = pick("xs3", xs, l_three, U8)
+        xs1 = pick("xs1", xs, l_offs, U8)
+        xs2 = pick("xs2", xs, l_two, U8)
+        xw3 = pick("xw3", xw, l_three, U32)
+
+        def cast_w(grouped, raw, b0, b1):
+            nc.scalar.copy(
+                grouped[:].rearrange("p (t b r j) -> p t b r j", t=4, r=8, j=4)[:, :, b0:b1],
+                raw[:].rearrange("p j (b t r) -> p t b r j", t=4, r=8),
+            )
+
+        def quantize(codes, scales, grouped, c0, c1):
+            nc.vector.quantize_mx(
+                out=codes[:, c0:c1].bitcast(FP8X4), scales=scales[:, c0:c1], in_=grouped[:, 4 * c0 : 4 * c1]
+            )
+
+        def planes(name):
+            return sb(name + "_codes", [P, N], U32), sb(name + "_scales", [P, N], U8)
+
+        def product(lhs, t, rhs, c0=0, c1=N):
+            bank = ps_mm.tile([P, N], F32, name="bank")
+            cols = slice(P * t, P * (t + 1))
+            nc.tensor.matmul_mx(
+                out=bank[:, 0 : c1 - c0],
+                lhsT=lhs[0][:, cols].bitcast(FP8X4),
+                lhsT_scale=lhs[1][:, cols],
+                rhs=rhs[0][:, c0:c1].bitcast(FP8X4),
+                rhs_scale=rhs[1][:, c0:c1],
+                start=True,
+                stop=True,
+            )
+            return bank
+
+        w3_g = sb("w3_g", [P, 4 * N], BF16)
+        cast_w(w3_g, w3_raw, 0, 16)
+        g_bank = ps_mm.tile([P, N], F32, name="bank")
+        nc.tensor.transpose(g_bank[:, 0:P], g_rows[:], ident[:])
+        gains = sb("gains", [P, 8], F32)
+        nc.scalar.copy(gains[:], g_bank[:, 0:8])
+        w3_q = planes("w3")
+        quantize(*w3_q, w3_g, 0, N)
+        xw1 = pick("xw1", xw, l_offs, U32)
+        xw2 = pick("xw2", xw, l_two, U32)
+
+        b_low = sb("b_low", [P, 4, N], BF16)
+
+        def make_b(t0):
+            for t in (t0, t0 + 1):
+                bank = product(w3_q, t, (xw3, xs3))
+                nc.scalar.activation(b_win[t][:, 0:N], bank[:], ACT.Copy, scale=gains[:, 4 + t : 5 + t])
+                nc.scalar.activation(b_low[:, t, :], bank[:], ACT.Copy, scale=gains[:, 4 + t : 5 + t])
+
+        make_b(0)
+
+        z2_rows = sb("z2_rows", [P, 4, N], BF16)
+
+        def median(name, t0, c0, c1, pa, pb):
+            width = c1 - c0
+            lo = sb(name + "_lo", [P, 2, width], BF16)
+            hi = sb(name + "_hi", [P, 2, width], BF16)
+            mid = sb(name + "_mid", [P, 2, width], BF16)
+            own = b_low[:, t0 : t0 + 2, c0:c1]
+            for e in range(2):
+                nc.vector.tensor_copy(pa[:, e, :], b_win[t0 + e][:].indirect(l_n3[:, c0 // 16 : c1 // 16]))
+            for e in range(2):
+                nc.vector.tensor_copy(pb[:, e, :], b_win[t0 + e][:].indirect(l_n4[:, c0 // 16 : c1 // 16]))
+            nc.vector.tensor_tensor(hi[:], own, pa, ALU.max)
+            nc.vector.tensor_tensor(lo[:], own, pa, ALU.min)
+            parts = [slice(0, width // 2), slice(width // 2, width)]
+            for part in parts:
+                nc.vector.tensor_tensor(mid[:, :, part], hi[:, :, part], pb[:, :, part], ALU.min)
+            for part in parts:
+                nc.vector.tensor_tensor(
+                    z2_rows[:, t0 : t0 + 2, c0 + part.start : c0 + part.stop], lo[:, :, part], mid[:, :, part], ALU.max
+                )
+
+        pa1 = sb("pa1", [P, 2, N], BF16)
+        pb1 = sb("pb1", [P, 2, N], BF16)
+        median("m1", 0, 0, N, pa1[:], pb1[:])
+
+        w1_g = sb("w1_g", [P, 4 * N], BF16)
+        cast_w(w1_g, w1_raw, 0, 16)
+        w1_q = planes("w1")
+        quantize(*w1_q, w1_g, 0, N)
+        w2_g = sb("w2_g", [P, 4 * N], BF16)
+        cast_w(w2_g, w2_raw, 0, 16)
+        w2_q = planes("w2")
+        quantize(*w2_q, w2_g, 0, N)
+        make_b(2)
+
+        pa2 = sb("pa2", [P, 2, HALF], BF16)
+        pb2 = sb("pb2", [P, 2, HALF], BF16)
+        median("m2", 2, 0, HALF, pa2[:], pb2[:])
+
+        d_neg = [d_win[t][:, N:WIDE] for t in range(4)]
+        cross = [sb("cross%d" % t, [P, N], F32) for t in range(4)]
+        z_back = [ps_back.tile([P, 2, HALF], F32, name="back") for x in range(2)]
+        z2_cols = {0: (0, HALF), 2: (HALF, HALF + P), 3: (HALF + P, N)}
+        z2_g = {h: sb("z2_g%d" % h, [P, 4 * (c[1] - c[0])], BF16) for h, c in z2_cols.items()}
+        z2_q = planes("z2")
+
+        def weave(engine_copy, h):
+            engine_copy(
+                z2_g[h][:].rearrange("p (c i t) -> p c t i", i=4, t=4),
+                z2_rows[:, :, z2_cols[h][0] : z2_cols[h][1]].rearrange("p t (c i) -> p c t i", i=4),
+            )
+
+        def quantize_z2(h):
+            cols = slice(*z2_cols[h])
+            nc.vector.quantize_mx(out=z2_q[0][:, cols].bitcast(FP8X4), scales=z2_q[1][:, cols], in_=z2_g[h][:])
+
+        def evacuate_pair(u):
+            banks = []
+            for t in (2 * u, 2 * u + 1):
+                bank = product(w1_q, t, (xw1, xs1))
+                nc.scalar.activation(y_win[t][:, 0:N], bank[:], ACT.Copy, scale=gains[:, t : t + 1])
+                bank = product(w2_q, t, (xw2, xs2))
+                nc.scalar.activation(d_win[t][:, 0:N], bank[:], ACT.Copy, scale=0.75)
+                nc.scalar.activation(d_neg[t], bank[:], ACT.Copy, scale=-0.75)
+
+        def gather_pair(u):
+            for t in (2 * u, 2 * u + 1):
+                nc.vector.tensor_tensor(y_win[t][:, N:WIDE], d_win[t][:].indirect(l_n2[:]), y_win[t][:, 0:N], ALU.mult)
+            for t in (2 * u, 2 * u + 1):
+                nc.vector.tensor_tensor(cross[t][:], y_win[t][:].indirect(l_n1[:]), d_neg[t], ALU.mult)
+
+        def add_turned(dst, first, second):
+            nc.tensor.matmul(dst, lhsT=first, rhs=ident[:], start=True, stop=False, is_transpose=True)
+            nc.tensor.matmul(dst, lhsT=second, rhs=ident[:], start=False, stop=True, is_transpose=True)
+
+        def sum_pair(u):
+            sums_z = [ps_sum.tile([P, 2, 2, P], F32, name="turned") for x in range(2)]
+            for e in range(2):
+                t = 2 * u + e
+                for x in range(2):
+                    for c in range(2):
+                        c0 = HALF * x + P * c
+                        add_turned(sums_z[x][:, c, e, :], y_win[t][:, N + c0 : N + c0 + P], cross[t][:, c0 : c0 + P])
+            for x in range(2):
+                turned = sums_z[x]
+                pairs = sb("pairs%d%d" % (u, x), [P, 2, P, 2], BF16)
+                nc.scalar.copy(pairs[:], turned[:].rearrange("i c e p -> i c p e"))
+                words = pairs[:].rearrange("i c p e -> i (c p e)").bitcast(F32)
+                for c in range(2):
+                    nc.tensor.transpose(z_back[x][:, u, P * c : P * (c + 1)], words[:, P * c : P * (c + 1)], ident[:])
+
+        evacuate_pair(0)
+        gather_pair(0)
+        evacuate_pair(1)
+        weave(nc.scalar.copy, 0)
+        gather_pair(1)
+        quantize_z2(0)
+        sum_pair(0)
+        sum_pair(1)
+        z_g = sb("z_g", [P, 4 * N], BF16)
+        z_words = z_g[:].bitcast(F32).rearrange("p (t m u) -> p t m u", t=4, u=2)
+        for x in range(2):
+            nc.scalar.copy(z_words[:, :, 64 * x : 64 * (x + 1), :], z_back[x][:].rearrange("p u (m t) -> p t m u", t=4))
+
+        pa3 = d_neg[2][:, 0:HALF].bitcast(BF16).rearrange("p (e c) -> p e c", e=2)
+        pb3 = d_neg[3][:, 0:HALF].bitcast(BF16).rearrange("p (e c) -> p e c", e=2)
+        median("m3", 2, HALF, N, pa3, pb3)
+        z_q = planes("z")
+        quantize(*z_q, z_g, 0, P)
+        for q in (2, 3):
+            weave(nc.vector.tensor_copy, q)
+        for q in (2, 3):
+            quantize_z2(q)
+        quantize(*z_q, z_g, P, 2 * P)
+        quantize(*z_q, z_g, 2 * P, 4 * P)
+
+        s_win = y_win
+        s_copy = [d_win[t][:, 0:N] for t in range(4)]
+        for h in range(2):
+            bank = product(z_q, 0, z2_q, HALF * h, HALF * (h + 1))
+            nc.scalar.activation(s_win[0][:, HALF * h : HALF * (h + 1)], bank[:, 0:HALF], ACT.Copy, scale=0.0625)
+        for t in range(1, 4):
+            bank = product(z_q, t, z2_q)
+            nc.scalar.activation(s_copy[t], bank[:], ACT.Copy, scale=0.0625)
+            nc.scalar.activation(s_win[t][:, 0:N], bank[:], ACT.Copy, scale=0.0625)
+        out_rows = out.rearrange("(p t) v -> p t v", t=4)
+        gap = [sb("gap%d" % t, [P, N], F32) for t in range(4)]
+        result = [sb("result%d" % t, [P, N], F32) for t in range(4)]
+        s6_0 = sb("s6_0", [P, N], F32)
+        nc.vector.tensor_copy(gap[0][:], s_win[0][:].indirect(l_n5[:]))
+        nc.vector.tensor_copy(s6_0[:], s_win[0][:].indirect(l_n6[:]))
+        nc.vector.tensor_tensor(gap[1][:], s_win[1][:].indirect(l_n5[:]), s_copy[1], ALU.subtract)
+        nc.vector.tensor_tensor(s_copy[1], s_win[0][:, 0:N], gap[0][:], ALU.max)
+        for t in (2, 3):
+            nc.vector.tensor_tensor(gap[t][:], s_win[t][:].indirect(l_n5[:]), s_copy[t], ALU.subtract)
+        nc.vector.tensor_tensor(result[0][:], s_copy[1], s6_0[:], ALU.min)
+        nc.sync.dma_start(out_rows[:, 0, :], result[0][:])
+        rise = cross
+        upper_t = [sb("upper_t%d" % t, [P, N], F32) for t in range(4)]
+
+        def lift(t):
+            nc.scalar.activation(rise[t][:], gap[t][:], ACT.Relu)
+            turned = ps_sum.tile([P, N], F32, name="turned")
+            for c in range(4):
+                cols = slice(P * c, P * (c + 1))
+                add_turned(turned[:, cols], s_win[t][:, cols], rise[t][:, cols])
+            return turned
+
+        def turn_back(t, turned):
+            nc.scalar.copy(upper_t[t][:], turned[:])
+            back = ps_back.tile([P, N], F32, name="back")
+            for c in range(4):
+                cols = slice(P * c, P * (c + 1))
+                nc.tensor.transpose(back[:, cols], upper_t[t][:, cols], ident[:])
+            return back
+
+        lifted = [lift(1), lift(2)]
+        backs = [turn_back(1, lifted[0])]
+        lifted.append(lift(3))
+        backs.append(turn_back(2, lifted[1]))
+        backs.append(turn_back(3, lifted[2]))
+        for t in range(1, 4):
+            nc.vector.tensor_copy(gap[t][:], s_win[t][:].indirect(l_n6[:]))
+        for t in range(1, 4):
+            nc.vector.tensor_tensor(result[t][:], backs[t - 1][:], gap[t][:], ALU.min)
+            nc.sync.dma_start(out_rows[:, t, :], result[t][:])

@@ -29,12 +29,12 @@ def tile_picked_twkcrossbmedminmx_none_p_kernel(
     with ExitStack() as ctx:
         lists = ctx.enter_context(tc.tile_pool(name="lists", bufs=1))
         keep = ctx.enter_context(tc.tile_pool(name="keep", bufs=1))
-        ps_mm = ctx.enter_context(tc.psum_pool(name="ps_mm", bufs=3))
-        ps_sum = ctx.enter_context(tc.psum_pool(name="ps_sum", bufs=2))
+        ps_mm = ctx.enter_context(tc.psum_pool(name="ps_mm", bufs=2))
+        ps_sum = ctx.enter_context(tc.psum_pool(name="ps_sum", bufs=3))
         ps_back = ctx.enter_context(tc.psum_pool(name="ps_back", bufs=3))
 
-        def sb(name, shape, dtype):
-            return keep.tile(shape, dtype, name=name, align_bytes=64)
+        def sb(name, shape, dtype, tag=None):
+            return keep.tile(shape, dtype, name=name, tag=tag or name, align_bytes=64)
 
         def load_list(name, src):
             tile = lists.tile([P, N // 16], U16, name=name)
@@ -44,17 +44,19 @@ def tile_picked_twkcrossbmedminmx_none_p_kernel(
         xs = sb("xs", [P, T], U8)
         nc.gpsimd.memset(xs[:].bitcast(I32), 0)
         l_three = load_list("l_three", three)
-        l_offs = load_list("l_offs", offs)
-        l_two = load_list("l_two", two)
         for q in range(4):
             nc.sync.dma_start(xs[32 * q : 32 * q + 4, :].bitcast(I32), x_scales[0, 4 * q : 4 * q + 4, :].bitcast(I32))
+        l_offs = load_list("l_offs", offs)
+        l_two = load_list("l_two", two)
+        xw = sb("xw", [P, T], U32)
+        nc.sync.dma_start(xw[:].bitcast(I32), x_words[0].rearrange("p n t -> p (n t)").bitcast(I32))
 
         def load_w(name, w, c0, c1):
             raw = sb(name, [P, 4, c1 - c0], F32)
             nc.sync.dma_start(raw[:], w.rearrange("(p j) c -> p j c", j=4)[:, :, c0:c1])
             return raw
 
-        w3_raw = load_w("w3_raw", w3, 0, N)
+        w3_raw = [load_w("w3_raw%d" % h, w3, HALF * h, HALF * (h + 1)) for h in range(2)]
         g_rows = sb("g_rows", [P, P], F32)
         nc.gpsimd.memset(g_rows[:], 0.0)
         for a, g in enumerate((ga, gb)):
@@ -62,8 +64,6 @@ def tile_picked_twkcrossbmedminmx_none_p_kernel(
                 g_rows[4 * a : 4 * a + 4, :].rearrange("t (b r) -> t b r", r=8),
                 g.rearrange("(b t r) o -> t b (r o)", t=4, r=8),
             )
-        xw = sb("xw", [P, T], U32)
-        nc.sync.dma_start(xw[:].bitcast(I32), x_words[0].rearrange("p n t -> p (n t)").bitcast(I32))
         l_n3 = load_list("l_n3", n3)
         l_n4 = load_list("l_n4", n4)
         w1_raw = load_w("w1_raw", w1, 0, N)
@@ -82,8 +82,8 @@ def tile_picked_twkcrossbmedminmx_none_p_kernel(
         for tile in b_win[:2]:
             nc.vector.memset(tile[:, N:WIDE], 0.0)
 
-        def pick(name, src, lst, dtype):
-            got = sb(name, [P, N], dtype)
+        def pick(name, src, lst, dtype, tag=None):
+            got = sb(name, [P, N], dtype, tag)
             nc.vector.tensor_copy(got[:], src[:].indirect(lst[:]))
             return got
 
@@ -121,7 +121,8 @@ def tile_picked_twkcrossbmedminmx_none_p_kernel(
             return bank
 
         w3_g = sb("w3_g", [P, 4 * N], BF16)
-        cast_w(w3_g, w3_raw, 0, 16)
+        for h in range(2):
+            cast_w(w3_g, w3_raw[h], 8 * h, 8 * h + 8)
         g_bank = ps_mm.tile([P, N], F32, name="bank")
         nc.tensor.transpose(g_bank[:, 0:P], g_rows[:], ident[:])
         gains = sb("gains", [P, 8], F32)
@@ -129,7 +130,7 @@ def tile_picked_twkcrossbmedminmx_none_p_kernel(
         w3_q = planes("w3")
         quantize(*w3_q, w3_g, 0, N)
         xw1 = pick("xw1", xw, l_offs, U32)
-        xw2 = pick("xw2", xw, l_two, U32)
+        xw2 = pick("xw2", xw, l_two, U32, "w3_g")
 
         b_low = sb("b_low", [P, 4, N], BF16)
 
@@ -190,8 +191,8 @@ def tile_picked_twkcrossbmedminmx_none_p_kernel(
 
         def weave(engine_copy, h):
             engine_copy(
-                z2_g[h][:].rearrange("p (c i t) -> p c t i", i=4, t=4),
-                z2_rows[:, :, z2_cols[h][0] : z2_cols[h][1]].rearrange("p t (c i) -> p c t i", i=4),
+                z2_g[h][:].rearrange("p (c t) -> p c t", t=4),
+                z2_rows[:, :, z2_cols[h][0] : z2_cols[h][1]].rearrange("p t c -> p c t"),
             )
 
         def quantize_z2(h):
@@ -213,18 +214,17 @@ def tile_picked_twkcrossbmedminmx_none_p_kernel(
             for t in (2 * u, 2 * u + 1):
                 nc.vector.tensor_tensor(cross[t][:], y_win[t][:].indirect(l_n1[:]), d_neg[t], ALU.mult)
 
-        def add_turned(dst, first, second):
-            nc.tensor.matmul(dst, lhsT=first, rhs=ident[:], start=True, stop=False, is_transpose=True)
-            nc.tensor.matmul(dst, lhsT=second, rhs=ident[:], start=False, stop=True, is_transpose=True)
+        def turn(dst, src, start, stop):
+            nc.tensor.matmul(dst, lhsT=src, rhs=ident[:], start=start, stop=stop, is_transpose=True)
 
         def sum_pair(u):
             sums_z = [ps_sum.tile([P, 2, 2, P], F32, name="turned") for x in range(2)]
-            for e in range(2):
-                t = 2 * u + e
-                for x in range(2):
-                    for c in range(2):
-                        c0 = HALF * x + P * c
-                        add_turned(sums_z[x][:, c, e, :], y_win[t][:, N + c0 : N + c0 + P], cross[t][:, c0 : c0 + P])
+            for a, terms in enumerate(([tile[:, N:WIDE] for tile in y_win], [tile[:] for tile in cross])):
+                for e in range(2):
+                    for x in range(2):
+                        for c in range(2):
+                            c0 = HALF * x + P * c
+                            turn(sums_z[x][:, c, e, :], terms[2 * u + e][:, c0 : c0 + P], a + e + c == 0, a + e + c == 3)
             for x in range(2):
                 turned = sums_z[x]
                 pairs = sb("pairs%d%d" % (u, x), [P, 2, P, 2], BF16)
@@ -249,20 +249,21 @@ def tile_picked_twkcrossbmedminmx_none_p_kernel(
         pa3 = d_neg[2][:, 0:HALF].bitcast(BF16).rearrange("p (e c) -> p e c", e=2)
         pb3 = d_neg[3][:, 0:HALF].bitcast(BF16).rearrange("p (e c) -> p e c", e=2)
         median("m3", 2, HALF, N, pa3, pb3)
-        z_q = planes("z")
-        quantize(*z_q, z_g, 0, P)
+        z_first = sb("z_codes0", [P, P], U32), sb("z_scales0", [P, P], U8)
+        quantize(*z_first, z_g, 0, P)
         for q in (2, 3):
             weave(nc.vector.tensor_copy, q)
         for q in (2, 3):
             quantize_z2(q)
+        z_q = sb("z_codes", [P, N], U32, "z2_g2"), sb("z_scales", [P, N], U8)
         quantize(*z_q, z_g, P, 2 * P)
         quantize(*z_q, z_g, 2 * P, 4 * P)
 
         s_win = y_win
         s_copy = [d_win[t][:, 0:N] for t in range(4)]
-        for h in range(2):
-            bank = product(z_q, 0, z2_q, HALF * h, HALF * (h + 1))
-            nc.scalar.activation(s_win[0][:, HALF * h : HALF * (h + 1)], bank[:, 0:HALF], ACT.Copy, scale=0.0625)
+        for c0, c1 in z2_cols.values():
+            bank = product(z_first, 0, z2_q, c0, c1)
+            nc.scalar.activation(s_win[0][:, c0:c1], bank[:, 0 : c1 - c0], ACT.Copy, scale=0.0625)
         for t in range(1, 4):
             bank = product(z_q, t, z2_q)
             nc.scalar.activation(s_copy[t], bank[:], ACT.Copy, scale=0.0625)
@@ -283,11 +284,12 @@ def tile_picked_twkcrossbmedminmx_none_p_kernel(
         upper_t = [sb("upper_t%d" % t, [P, N], F32) for t in range(4)]
 
         def lift(t):
-            nc.scalar.activation(rise[t][:], gap[t][:], ACT.Relu)
             turned = ps_sum.tile([P, N], F32, name="turned")
-            for c in range(4):
-                cols = slice(P * c, P * (c + 1))
-                add_turned(turned[:, cols], s_win[t][:, cols], rise[t][:, cols])
+            nc.scalar.activation(rise[t][:], gap[t][:], ACT.Relu)
+            for a, term in enumerate((s_win[t], rise[t])):
+                for c in range(4):
+                    cols = slice(P * c, P * (c + 1))
+                    turn(turned[:, cols], term[:, cols], a + c == 0, a + c == 4)
             return turned
 
         def turn_back(t, turned):
@@ -298,13 +300,11 @@ def tile_picked_twkcrossbmedminmx_none_p_kernel(
                 nc.tensor.transpose(back[:, cols], upper_t[t][:, cols], ident[:])
             return back
 
-        lifted = [lift(1), lift(2)]
-        backs = [turn_back(1, lifted[0])]
-        lifted.append(lift(3))
-        backs.append(turn_back(2, lifted[1]))
-        backs.append(turn_back(3, lifted[2]))
+        lifted = [lift(t) for t in range(1, 4)]
+        backs = [turn_back(t, lifted[t - 1]) for t in range(1, 4)]
         for t in range(1, 4):
             nc.vector.tensor_copy(gap[t][:], s_win[t][:].indirect(l_n6[:]))
         for t in range(1, 4):
-            nc.vector.tensor_tensor(result[t][:], backs[t - 1][:], gap[t][:], ALU.min)
-            nc.sync.dma_start(out_rows[:, t, :], result[t][:])
+            for c0, c1 in ((0, N),) if t < 3 else ((0, HALF), (HALF, N)):
+                nc.vector.tensor_tensor(result[t][:, c0:c1], backs[t - 1][:, c0:c1], gap[t][:, c0:c1], ALU.min)
+                nc.sync.dma_start(out_rows[:, t, c0:c1], result[t][:, c0:c1])

@@ -165,7 +165,7 @@ def tile_picked_twkcrossbmedminmx_none_p_kernel(
                 )
 
         pa1 = sb("pa1", [P, 2, N], BF16)
-        pb1 = sb("pb1", [P, 2, N], BF16)
+        pb1 = sb("pb1", [P, 2, N], F32)
         median("m1", 0, 0, N, pa1[:], pb1[:])
 
         w1_g = sb("w1_g", [P, 4 * N], BF16)
@@ -179,7 +179,7 @@ def tile_picked_twkcrossbmedminmx_none_p_kernel(
         make_b(2)
 
         pa2 = sb("pa2", [P, 2, HALF], BF16)
-        pb2 = sb("pb2", [P, 2, HALF], BF16)
+        pb2 = sb("pb2", [P, 2, HALF], F32)
         median("m2", 2, 0, HALF, pa2[:], pb2[:])
 
         d_neg = [d_win[t][:, N:WIDE] for t in range(4)]
@@ -247,23 +247,23 @@ def tile_picked_twkcrossbmedminmx_none_p_kernel(
             nc.scalar.copy(z_words[:, :, 64 * x : 64 * (x + 1), :], z_back[x][:].rearrange("p u (m t) -> p t m u", t=4))
 
         pa3 = d_neg[2][:, 0:HALF].bitcast(BF16).rearrange("p (e c) -> p e c", e=2)
-        pb3 = d_neg[3][:, 0:HALF].bitcast(BF16).rearrange("p (e c) -> p e c", e=2)
+        pb3 = d_neg[3].rearrange("p (e c) -> p e c", e=2)
         median("m3", 2, HALF, N, pa3, pb3)
-        z_first = sb("z_codes0", [P, P], U32), sb("z_scales0", [P, P], U8)
-        quantize(*z_first, z_g, 0, P)
+        z_q = planes("z")
+        quantize(*z_q, z_g, 0, P)
         for q in (2, 3):
             weave(nc.vector.tensor_copy, q)
         for q in (2, 3):
             quantize_z2(q)
-        z_q = sb("z_codes", [P, N], U32, "z2_g2"), sb("z_scales", [P, N], U8)
         quantize(*z_q, z_g, P, 2 * P)
         quantize(*z_q, z_g, 2 * P, 4 * P)
 
         s_win = y_win
         s_copy = [d_win[t][:, 0:N] for t in range(4)]
-        for c0, c1 in z2_cols.values():
-            bank = product(z_first, 0, z2_q, c0, c1)
-            nc.scalar.activation(s_win[0][:, c0:c1], bank[:, 0 : c1 - c0], ACT.Copy, scale=0.0625)
+        for h in range(2):
+            bank = product(z_q, 0, z2_q, HALF * h, HALF * (h + 1))
+            nc.scalar.activation(s_win[0][:, HALF * h : HALF * (h + 1)], bank[:, 0:HALF], ACT.Copy, scale=0.0625)
+            nc.scalar.activation(s_copy[0][:, HALF * h : HALF * (h + 1)], bank[:, 0:HALF], ACT.Copy, scale=0.0625)
         for t in range(1, 4):
             bank = product(z_q, t, z2_q)
             nc.scalar.activation(s_copy[t], bank[:], ACT.Copy, scale=0.0625)
@@ -271,15 +271,10 @@ def tile_picked_twkcrossbmedminmx_none_p_kernel(
         out_rows = out.rearrange("(p t) v -> p t v", t=4)
         gap = [sb("gap%d" % t, [P, N], F32) for t in range(4)]
         result = [sb("result%d" % t, [P, N], F32) for t in range(4)]
-        s6_0 = sb("s6_0", [P, N], F32)
-        nc.vector.tensor_copy(gap[0][:], s_win[0][:].indirect(l_n5[:]))
-        nc.vector.tensor_copy(s6_0[:], s_win[0][:].indirect(l_n6[:]))
-        nc.vector.tensor_tensor(gap[1][:], s_win[1][:].indirect(l_n5[:]), s_copy[1], ALU.subtract)
-        nc.vector.tensor_tensor(s_copy[1], s_win[0][:, 0:N], gap[0][:], ALU.max)
-        for t in (2, 3):
+        s6 = [sb("s6_0", [P, N], F32)] + gap[1:]
+        nc.vector.tensor_copy(s6[0][:], s_win[0][:].indirect(l_n6[:]))
+        for t in range(4):
             nc.vector.tensor_tensor(gap[t][:], s_win[t][:].indirect(l_n5[:]), s_copy[t], ALU.subtract)
-        nc.vector.tensor_tensor(result[0][:], s_copy[1], s6_0[:], ALU.min)
-        nc.sync.dma_start(out_rows[:, 0, :], result[0][:])
         rise = cross
         upper_t = [sb("upper_t%d" % t, [P, N], F32) for t in range(4)]
 
@@ -300,11 +295,13 @@ def tile_picked_twkcrossbmedminmx_none_p_kernel(
                 nc.tensor.transpose(back[:, cols], upper_t[t][:, cols], ident[:])
             return back
 
-        lifted = [lift(t) for t in range(1, 4)]
-        backs = [turn_back(t, lifted[t - 1]) for t in range(1, 4)]
+        lifted = [lift(t) for t in range(3)]
+        backs = [turn_back(0, lifted[0])]
+        lifted.append(lift(3))
+        backs.extend(turn_back(t, lifted[t]) for t in range(1, 4))
         for t in range(1, 4):
             nc.vector.tensor_copy(gap[t][:], s_win[t][:].indirect(l_n6[:]))
-        for t in range(1, 4):
+        for t in range(4):
             for c0, c1 in ((0, N),) if t < 3 else ((0, HALF), (HALF, N)):
-                nc.vector.tensor_tensor(result[t][:, c0:c1], backs[t - 1][:, c0:c1], gap[t][:, c0:c1], ALU.min)
+                nc.vector.tensor_tensor(result[t][:, c0:c1], backs[t][:, c0:c1], s6[t][:, c0:c1], ALU.min)
                 nc.sync.dma_start(out_rows[:, t, c0:c1], result[t][:, c0:c1])

@@ -48,6 +48,7 @@ def tile_picked_twkcrossbmedminmx_none_p_kernel(
             nc.sync.dma_start(xs[32 * q : 32 * q + 4, :].bitcast(I32), x_scales[0, 4 * q : 4 * q + 4, :].bitcast(I32))
         l_offs = load_list("l_offs", offs)
         l_two = load_list("l_two", two)
+
         xw = sb("xw", [P, T], U32)
         nc.sync.dma_start(xw[:].bitcast(I32), x_words[0].rearrange("p n t -> p (n t)").bitcast(I32))
 
@@ -56,7 +57,7 @@ def tile_picked_twkcrossbmedminmx_none_p_kernel(
             nc.sync.dma_start(raw[:], w.rearrange("(p j) c -> p j c", j=4)[:, :, c0:c1])
             return raw
 
-        w3_raw = [load_w("w3_raw%d" % h, w3, HALF * h, HALF * (h + 1)) for h in range(2)]
+        w3_raw = load_w("w3_raw", w3, 0, N)
         g_rows = sb("g_rows", [P, P], F32)
         nc.gpsimd.memset(g_rows[:], 0.0)
         for a, g in enumerate((ga, gb)):
@@ -79,8 +80,10 @@ def tile_picked_twkcrossbmedminmx_none_p_kernel(
         b_win = [sb("b_win%d" % t, [P, WIDE if t < 2 else N], F32) for t in range(4)]
         d_win = [sb("d_win%d" % t, [P, WIDE], F32) for t in range(4)]
         y_win = [sb("y_win%d" % t, [P, WIDE], F32) for t in range(4)]
-        for tile in b_win[:2]:
+        for tile in b_win[:2] + y_win[:2]:
             nc.vector.memset(tile[:, N:WIDE], 0.0)
+        for tile in y_win[2:]:
+            nc.gpsimd.memset(tile[:, N:WIDE], 0.0)
 
         def pick(name, src, lst, dtype, tag=None):
             got = sb(name, [P, N], dtype, tag)
@@ -92,15 +95,15 @@ def tile_picked_twkcrossbmedminmx_none_p_kernel(
         xs2 = pick("xs2", xs, l_two, U8)
         xw3 = pick("xw3", xw, l_three, U32)
 
-        def cast_w(grouped, raw, b0, b1):
-            nc.scalar.copy(
-                grouped[:].rearrange("p (t b r j) -> p t b r j", t=4, r=8, j=4)[:, :, b0:b1],
-                raw[:].rearrange("p j (b t r) -> p t b r j", t=4, r=8),
-            )
+        def cast_w(grouped, raw, t0=0, count=4):
+            dst = grouped[:].rearrange("p (t b h i j) -> p t b h j i", t=count, h=2, i=4, j=4)
+            src = raw[:].rearrange("p j (b t h i) -> p t b h j i", t=4, h=2, i=4)
+            for t in range(count):
+                nc.scalar.copy(dst[:, t], src[:, t0 + t])
 
-        def quantize(codes, scales, grouped, c0, c1):
+        def quantize(codes, scales, grouped, c0, c1, first=0):
             nc.vector.quantize_mx(
-                out=codes[:, c0:c1].bitcast(FP8X4), scales=scales[:, c0:c1], in_=grouped[:, 4 * c0 : 4 * c1]
+                out=codes[:, c0:c1].bitcast(FP8X4), scales=scales[:, c0:c1], in_=grouped[:, 4 * (c0 - first) : 4 * (c1 - first)]
             )
 
         def planes(name):
@@ -120,17 +123,18 @@ def tile_picked_twkcrossbmedminmx_none_p_kernel(
             )
             return bank
 
-        w3_g = sb("w3_g", [P, 4 * N], BF16)
-        for h in range(2):
-            cast_w(w3_g, w3_raw[h], 8 * h, 8 * h + 8)
+        w3_g = [sb("w3_g%d" % u, [P, 2 * N], BF16) for u in range(2)]
+        for u in range(2):
+            cast_w(w3_g[u], w3_raw, 2 * u, 2)
         g_bank = ps_mm.tile([P, N], F32, name="bank")
         nc.tensor.transpose(g_bank[:, 0:P], g_rows[:], ident[:])
         gains = sb("gains", [P, 8], F32)
         nc.scalar.copy(gains[:], g_bank[:, 0:8])
         w3_q = planes("w3")
-        quantize(*w3_q, w3_g, 0, N)
+        for u in range(2):
+            quantize(*w3_q, w3_g[u], HALF * u, HALF * (u + 1), HALF * u)
         xw1 = pick("xw1", xw, l_offs, U32)
-        xw2 = pick("xw2", xw, l_two, U32, "w3_g")
+        xw2 = pick("xw2", xw, l_two, U32, "w3_g0")
 
         b_low = sb("b_low", [P, 4, N], BF16)
 
@@ -144,11 +148,11 @@ def tile_picked_twkcrossbmedminmx_none_p_kernel(
 
         z2_rows = sb("z2_rows", [P, 4, N], BF16)
 
-        def median(name, t0, c0, c1, pa, pb):
+        def median(name, t0, c0, c1, pa, pb, mid_tag=None):
             width = c1 - c0
             lo = sb(name + "_lo", [P, 2, width], BF16)
             hi = sb(name + "_hi", [P, 2, width], BF16)
-            mid = sb(name + "_mid", [P, 2, width], BF16)
+            mid = sb(name + "_mid", [P, 2, width], BF16, mid_tag)
             own = b_low[:, t0 : t0 + 2, c0:c1]
             for e in range(2):
                 nc.vector.tensor_copy(pa[:, e, :], b_win[t0 + e][:].indirect(l_n3[:, c0 // 16 : c1 // 16]))
@@ -165,24 +169,25 @@ def tile_picked_twkcrossbmedminmx_none_p_kernel(
                 )
 
         pa1 = sb("pa1", [P, 2, N], BF16)
-        pb1 = sb("pb1", [P, 2, N], F32)
+        pb1 = sb("pb1", [P, 2, N], BF16)
         median("m1", 0, 0, N, pa1[:], pb1[:])
 
         w1_g = sb("w1_g", [P, 4 * N], BF16)
-        cast_w(w1_g, w1_raw, 0, 16)
+        cast_w(w1_g, w1_raw)
         w1_q = planes("w1")
         quantize(*w1_q, w1_g, 0, N)
         w2_g = sb("w2_g", [P, 4 * N], BF16)
-        cast_w(w2_g, w2_raw, 0, 16)
+        cast_w(w2_g, w2_raw)
         w2_q = planes("w2")
         quantize(*w2_q, w2_g, 0, N)
         make_b(2)
 
         pa2 = sb("pa2", [P, 2, HALF], BF16)
-        pb2 = sb("pb2", [P, 2, HALF], F32)
+        pb2 = sb("pb2", [P, 2, HALF], BF16)
         median("m2", 2, 0, HALF, pa2[:], pb2[:])
 
         d_neg = [d_win[t][:, N:WIDE] for t in range(4)]
+        straight = [sb("straight%d" % t, [P, N], F32) for t in range(4)]
         cross = [sb("cross%d" % t, [P, N], F32) for t in range(4)]
         z_back = [ps_back.tile([P, 2, HALF], F32, name="back") for x in range(2)]
         z2_cols = {0: (0, HALF), 2: (HALF, HALF + P), 3: (HALF + P, N)}
@@ -191,8 +196,8 @@ def tile_picked_twkcrossbmedminmx_none_p_kernel(
 
         def weave(engine_copy, h):
             engine_copy(
-                z2_g[h][:].rearrange("p (c t) -> p c t", t=4),
-                z2_rows[:, :, z2_cols[h][0] : z2_cols[h][1]].rearrange("p t c -> p c t"),
+                z2_g[h][:].rearrange("p (c i t) -> p c t i", i=4, t=4),
+                z2_rows[:, :, z2_cols[h][0] : z2_cols[h][1]].rearrange("p t (c i) -> p c t i", i=4),
             )
 
         def quantize_z2(h):
@@ -210,7 +215,7 @@ def tile_picked_twkcrossbmedminmx_none_p_kernel(
 
         def gather_pair(u):
             for t in (2 * u, 2 * u + 1):
-                nc.vector.tensor_tensor(y_win[t][:, N:WIDE], d_win[t][:].indirect(l_n2[:]), y_win[t][:, 0:N], ALU.mult)
+                nc.vector.tensor_tensor(straight[t][:], d_win[t][:].indirect(l_n2[:]), y_win[t][:, 0:N], ALU.mult)
             for t in (2 * u, 2 * u + 1):
                 nc.vector.tensor_tensor(cross[t][:], y_win[t][:].indirect(l_n1[:]), d_neg[t], ALU.mult)
 
@@ -219,7 +224,7 @@ def tile_picked_twkcrossbmedminmx_none_p_kernel(
 
         def sum_pair(u):
             sums_z = [ps_sum.tile([P, 2, 2, P], F32, name="turned") for x in range(2)]
-            for a, terms in enumerate(([tile[:, N:WIDE] for tile in y_win], [tile[:] for tile in cross])):
+            for a, terms in enumerate(([tile[:] for tile in straight], [tile[:] for tile in cross])):
                 for e in range(2):
                     for x in range(2):
                         for c in range(2):
@@ -241,27 +246,32 @@ def tile_picked_twkcrossbmedminmx_none_p_kernel(
         quantize_z2(0)
         sum_pair(0)
         sum_pair(1)
-        z_g = sb("z_g", [P, 4 * N], BF16)
-        z_words = z_g[:].bitcast(F32).rearrange("p (t m u) -> p t m u", t=4, u=2)
-        for x in range(2):
-            nc.scalar.copy(z_words[:, :, 64 * x : 64 * (x + 1), :], z_back[x][:].rearrange("p u (m t) -> p t m u", t=4))
+        z_g0 = sb("z_g0", [P, N], BF16)
+        z_g = sb("z_g", [P, 3 * N], BF16)
+        for grouped, t0, t1 in ((z_g0, 0, 1), (z_g, 1, 4)):
+            z_words = grouped[:].bitcast(F32).rearrange("p (t m u) -> p t m u", m=P, u=2)
+            for x in range(2):
+                nc.scalar.copy(
+                    z_words[:, :, 64 * x : 64 * (x + 1), :], z_back[x][:].rearrange("p u (m t) -> p t m u", t=4)[:, t0:t1]
+                )
+        z_first = sb("z_codes0", [P, P], U32), sb("z_scales0", [P, P], U8)
+        quantize(*z_first, z_g0, 0, P)
 
-        pa3 = d_neg[2][:, 0:HALF].bitcast(BF16).rearrange("p (e c) -> p e c", e=2)
-        pb3 = d_neg[3].rearrange("p (e c) -> p e c", e=2)
-        median("m3", 2, HALF, N, pa3, pb3)
-        z_q = planes("z")
-        quantize(*z_q, z_g, 0, P)
+        pa3 = d_neg[3][:, HALF:N].bitcast(BF16).rearrange("p (e c) -> p e c", e=2)
+        pb3 = d_neg[3][:, 0:HALF].bitcast(BF16).rearrange("p (e c) -> p e c", e=2)
+        median("m3", 2, HALF, N, pa3, pb3, "z_g0")
         for q in (2, 3):
             weave(nc.vector.tensor_copy, q)
         for q in (2, 3):
             quantize_z2(q)
-        quantize(*z_q, z_g, P, 2 * P)
-        quantize(*z_q, z_g, 2 * P, 4 * P)
+        z_q = sb("z_codes", [P, N], U32, "z2_g2"), sb("z_scales", [P, N], U8)
+        quantize(*z_q, z_g, P, 2 * P, P)
+        quantize(*z_q, z_g, 2 * P, 4 * P, P)
 
         s_win = y_win
         s_copy = [d_win[t][:, 0:N] for t in range(4)]
         for h in range(2):
-            bank = product(z_q, 0, z2_q, HALF * h, HALF * (h + 1))
+            bank = product(z_first, 0, z2_q, HALF * h, HALF * (h + 1))
             nc.scalar.activation(s_win[0][:, HALF * h : HALF * (h + 1)], bank[:, 0:HALF], ACT.Copy, scale=0.0625)
             nc.scalar.activation(s_copy[0][:, HALF * h : HALF * (h + 1)], bank[:, 0:HALF], ACT.Copy, scale=0.0625)
         for t in range(1, 4):

from contextlib import ExitStack

import concourse.mybir as mybir
from concourse.masks import make_identity

K, T, S, V, H = 512, 2048, 512, 512, 512
FLOPS = 4 * 2 * 512 * 512 * 512

F32 = mybir.dt.float32
BF16 = mybir.dt.bfloat16
I32 = mybir.dt.int32
U32 = mybir.dt.uint32
U16 = mybir.dt.uint16
U8 = mybir.dt.uint8
FP8X4 = mybir.dt.float8_e4m3fn_x4
ALU = mybir.AluOpType
ACT = mybir.ActivationFunctionType

P = 128
N = 512
HALF = 256
WIDE = 1024


def tile_picked_twkcrossbmedminmx_none_p_kernel(
    tc, x_words, x_scales, w1, w2, w3, ga, gb, offs, two, n1, n2, three, n3, n4, n5, n6, out
):
    nc = tc.nc
    with ExitStack() as ctx:
        lists = ctx.enter_context(tc.tile_pool(name="lists", bufs=1))
        keep = ctx.enter_context(tc.tile_pool(name="keep", bufs=1))
        ps_mm = ctx.enter_context(tc.psum_pool(name="ps_mm", bufs=2))
        ps_sum = ctx.enter_context(tc.psum_pool(name="ps_sum", bufs=3))
        ps_back = ctx.enter_context(tc.psum_pool(name="ps_back", bufs=3))

        def sb(name, shape, dtype, tag=None):
            return keep.tile(shape, dtype, name=name, tag=tag or name, align_bytes=64)

        def load_list(name, src):
            tile = lists.tile([P, N // 16], U16, name=name)
            nc.sync.dma_start(tile[:], src)
            return tile

        xs = sb("xs", [P, T], U8)
        nc.gpsimd.memset(xs[:].bitcast(I32), 0)
        l_three = load_list("l_three", three)
        for q in range(4):
            nc.sync.dma_start(xs[32 * q : 32 * q + 4, :].bitcast(I32), x_scales[0, 4 * q : 4 * q + 4, :].bitcast(I32))
        l_offs = load_list("l_offs", offs)
        l_two = load_list("l_two", two)

        xw = sb("xw", [P, T], U32)
        nc.sync.dma_start(xw[:].bitcast(I32), x_words[0].rearrange("p n t -> p (n t)").bitcast(I32))

        def load_w(name, w, c0, c1):
            raw = sb(name, [P, 4, c1 - c0], F32)
            nc.sync.dma_start(raw[:], w.rearrange("(p j) c -> p j c", j=4)[:, :, c0:c1])
            return raw

        w3_raw = load_w("w3_raw", w3, 0, N)
        g_rows = sb("g_rows", [P, P], F32)
        nc.gpsimd.memset(g_rows[:], 0.0)
        for a, g in enumerate((ga, gb)):
            nc.sync.dma_start(
                g_rows[4 * a : 4 * a + 4, :].rearrange("t (b r) -> t b r", r=8),
                g.rearrange("(b t r) o -> t b (r o)", t=4, r=8),
            )
        l_n3 = load_list("l_n3", n3)
        l_n4 = load_list("l_n4", n4)
        w1_raw = load_w("w1_raw", w1, 0, N)
        w2_raw = load_w("w2_raw", w2, 0, N)
        l_n2 = load_list("l_n2", n2)
        l_n1 = load_list("l_n1", n1)
        l_n5 = load_list("l_n5", n5)
        l_n6 = load_list("l_n6", n6)

        ident = sb("ident", [P, P], F32)
        make_identity(nc, ident[:])

        b_win = [sb("b_win%d" % t, [P, WIDE if t < 2 else N], F32) for t in range(4)]
        d_win = [sb("d_win%d" % t, [P, WIDE], F32) for t in range(4)]
        y_win = [sb("y_win%d" % t, [P, WIDE], F32) for t in range(4)]
        for tile in b_win[:2] + y_win[:2]:
            nc.vector.memset(tile[:, N:WIDE], 0.0)
        for tile in y_win[2:]:
            nc.gpsimd.memset(tile[:, N:WIDE], 0.0)

        def pick(name, src, lst, dtype, tag=None):
            got = sb(name, [P, N], dtype, tag)
            nc.vector.tensor_copy(got[:], src[:].indirect(lst[:]))
            return got

        xs3 = pick("xs3", xs, l_three, U8)
        xs1 = pick("xs1", xs, l_offs, U8)
        xs2 = pick("xs2", xs, l_two, U8)
        xw3 = pick("xw3", xw, l_three, U32)

        def cast_w(grouped, raw, t0=0, count=4):
            dst = grouped[:].rearrange("p (t b h i j) -> p t b h j i", t=count, h=2, i=4, j=4)
            src = raw[:].rearrange("p j (b t h i) -> p t b h j i", t=4, h=2, i=4)
            for t in range(count):
                nc.scalar.copy(dst[:, t], src[:, t0 + t])

        def quantize(codes, scales, grouped, c0, c1, first=0):
            nc.vector.quantize_mx(
                out=codes[:, c0:c1].bitcast(FP8X4), scales=scales[:, c0:c1], in_=grouped[:, 4 * (c0 - first) : 4 * (c1 - first)]
            )

        def planes(name):
            return sb(name + "_codes", [P, N], U32), sb(name + "_scales", [P, N], U8)

        def product(lhs, t, rhs, c0=0, c1=N):
            bank = ps_mm.tile([P, N], F32, name="bank")
            cols = slice(P * t, P * (t + 1))
            nc.tensor.matmul_mx(
                out=bank[:, 0 : c1 - c0],
                lhsT=lhs[0][:, cols].bitcast(FP8X4),
                lhsT_scale=lhs[1][:, cols],
                rhs=rhs[0][:, c0:c1].bitcast(FP8X4),
                rhs_scale=rhs[1][:, c0:c1],
                start=True,
                stop=True,
            )
            return bank

        w3_g = [sb("w3_g%d" % u, [P, 2 * N], BF16) for u in range(2)]
        for u in range(2):
            cast_w(w3_g[u], w3_raw, 2 * u, 2)
        g_bank = ps_mm.tile([P, N], F32, name="bank")
        nc.tensor.transpose(g_bank[:, 0:P], g_rows[:], ident[:])
        gains = sb("gains", [P, 8], F32)
        nc.scalar.copy(gains[:], g_bank[:, 0:8])
        w3_q = planes("w3")
        for u in range(2):
            quantize(*w3_q, w3_g[u], HALF * u, HALF * (u + 1), HALF * u)
        xw1 = pick("xw1", xw, l_offs, U32)
        xw2 = pick("xw2", xw, l_two, U32, "w3_g0")

        b_low = sb("b_low", [P, 4, N], BF16)

        def make_b(t0):
            for t in (t0, t0 + 1):
                bank = product(w3_q, t, (xw3, xs3))
                nc.scalar.activation(b_win[t][:, 0:N], bank[:], ACT.Copy, scale=gains[:, 4 + t : 5 + t])
                nc.scalar.activation(b_low[:, t, :], bank[:], ACT.Copy, scale=gains[:, 4 + t : 5 + t])

        make_b(0)

        z2_rows = sb("z2_rows", [P, 4, N], BF16)

        def median(name, t0, c0, c1, pa, pb, mid_tag=None):
            width = c1 - c0
            lo = sb(name + "_lo", [P, 2, width], BF16)
            hi = sb(name + "_hi", [P, 2, width], BF16)
            mid = sb(name + "_mid", [P, 2, width], BF16, mid_tag)
            own = b_low[:, t0 : t0 + 2, c0:c1]
            for e in range(2):
                nc.vector.tensor_copy(pa[:, e, :], b_win[t0 + e][:].indirect(l_n3[:, c0 // 16 : c1 // 16]))
            for e in range(2):
                nc.vector.tensor_copy(pb[:, e, :], b_win[t0 + e][:].indirect(l_n4[:, c0 // 16 : c1 // 16]))
            nc.vector.tensor_tensor(hi[:], own, pa, ALU.max)
            nc.vector.tensor_tensor(lo[:], own, pa, ALU.min)
            parts = [slice(0, width // 2), slice(width // 2, width)]
            for part in parts:
                nc.vector.tensor_tensor(mid[:, :, part], hi[:, :, part], pb[:, :, part], ALU.min)
            for part in parts:
                nc.vector.tensor_tensor(
                    z2_rows[:, t0 : t0 + 2, c0 + part.start : c0 + part.stop], lo[:, :, part], mid[:, :, part], ALU.max
                )

        pa1 = sb("pa1", [P, 2, N], BF16)
        pb1 = sb("pb1", [P, 2, N], BF16)
        median("m1", 0, 0, N, pa1[:], pb1[:])

        w1_g = sb("w1_g", [P, 4 * N], BF16)
        cast_w(w1_g, w1_raw)
        w1_q = planes("w1")
        quantize(*w1_q, w1_g, 0, N)
        w2_g = sb("w2_g", [P, 4 * N], BF16)
        cast_w(w2_g, w2_raw)
        w2_q = planes("w2")
        quantize(*w2_q, w2_g, 0, N)
        make_b(2)

        pa2 = sb("pa2", [P, 2, HALF], BF16)
        pb2 = sb("pb2", [P, 2, HALF], BF16)
        median("m2", 2, 0, HALF, pa2[:], pb2[:])

        d_neg = [d_win[t][:, N:WIDE] for t in range(4)]
        straight = [sb("straight%d" % t, [P, N], F32) for t in range(4)]
        cross = [sb("cross%d" % t, [P, N], F32) for t in range(4)]
        z_back = [ps_back.tile([P, 2, HALF], F32, name="back") for x in range(2)]
        z2_cols = {0: (0, HALF), 2: (HALF, HALF + P), 3: (HALF + P, N)}
        z2_g = {h: sb("z2_g%d" % h, [P, 4 * (c[1] - c[0])], BF16) for h, c in z2_cols.items()}
        z2_q = planes("z2")

        def weave(engine_copy, h):
            engine_copy(
                z2_g[h][:].rearrange("p (c i t) -> p c t i", i=4, t=4),
                z2_rows[:, :, z2_cols[h][0] : z2_cols[h][1]].rearrange("p t (c i) -> p c t i", i=4),
            )

        def quantize_z2(h):
            cols = slice(*z2_cols[h])
            nc.vector.quantize_mx(out=z2_q[0][:, cols].bitcast(FP8X4), scales=z2_q[1][:, cols], in_=z2_g[h][:])

        def evacuate_pair(u):
            banks = []
            for t in (2 * u, 2 * u + 1):
                bank = product(w1_q, t, (xw1, xs1))
                nc.scalar.activation(y_win[t][:, 0:N], bank[:], ACT.Copy, scale=gains[:, t : t + 1])
                bank = product(w2_q, t, (xw2, xs2))
                nc.scalar.activation(d_win[t][:, 0:N], bank[:], ACT.Copy, scale=0.75)
                nc.scalar.activation(d_neg[t], bank[:], ACT.Copy, scale=-0.75)

        def gather_pair(u):
            for t in (2 * u, 2 * u + 1):
                nc.vector.tensor_tensor(straight[t][:], d_win[t][:].indirect(l_n2[:]), y_win[t][:, 0:N], ALU.mult)
            for t in (2 * u, 2 * u + 1):
                nc.vector.tensor_tensor(cross[t][:], y_win[t][:].indirect(l_n1[:]), d_neg[t], ALU.mult)

        def turn(dst, src, start, stop):
            nc.tensor.matmul(dst, lhsT=src, rhs=ident[:], start=start, stop=stop, is_transpose=True)

        def sum_pair(u):
            sums_z = [ps_sum.tile([P, 2, 2, P], F32, name="turned") for x in range(2)]
            for a, terms in enumerate(([tile[:] for tile in straight], [tile[:] for tile in cross])):
                for e in range(2):
                    for x in range(2):
                        for c in range(2):
                            c0 = HALF * x + P * c
                            turn(sums_z[x][:, c, e, :], terms[2 * u + e][:, c0 : c0 + P], a + e + c == 0, a + e + c == 3)
            for x in range(2):
                turned = sums_z[x]
                pairs = sb("pairs%d%d" % (u, x), [P, 2, P, 2], BF16)
                nc.scalar.copy(pairs[:], turned[:].rearrange("i c e p -> i c p e"))
                words = pairs[:].rearrange("i c p e -> i (c p e)").bitcast(F32)
                for c in range(2):
                    nc.tensor.transpose(z_back[x][:, u, P * c : P * (c + 1)], words[:, P * c : P * (c + 1)], ident[:])

        evacuate_pair(0)
        gather_pair(0)
        evacuate_pair(1)
        weave(nc.scalar.copy, 0)
        gather_pair(1)
        quantize_z2(0)
        sum_pair(0)
        sum_pair(1)
        z_g0 = sb("z_g0", [P, N], BF16)
        z_g = sb("z_g", [P, 3 * N], BF16)
        for grouped, t0, t1 in ((z_g0, 0, 1), (z_g, 1, 4)):
            z_words = grouped[:].bitcast(F32).rearrange("p (t m u) -> p t m u", m=P, u=2)
            for x in range(2):
                nc.scalar.copy(
                    z_words[:, :, 64 * x : 64 * (x + 1), :], z_back[x][:].rearrange("p u (m t) -> p t m u", t=4)[:, t0:t1]
                )
        z_first = sb("z_codes0", [P, P], U32), sb("z_scales0", [P, P], U8)
        quantize(*z_first, z_g0, 0, P)

        pa3 = d_neg[3][:, HALF:N].bitcast(BF16).rearrange("p (e c) -> p e c", e=2)
        pb3 = d_neg[3][:, 0:HALF].bitcast(BF16).rearrange("p (e c) -> p e c", e=2)
        median("m3", 2, HALF, N, pa3, pb3, "z_g0")
        for q in (2, 3):
            weave(nc.vector.tensor_copy, q)
        for q in (2, 3):
            quantize_z2(q)
        z_q = sb("z_codes", [P, N], U32, "z2_g2"), sb("z_scales", [P, N], U8)
        quantize(*z_q, z_g, P, 2 * P, P)
        quantize(*z_q, z_g, 2 * P, 4 * P, P)

        s_win = y_win
        s_copy = [d_win[t][:, 0:N] for t in range(4)]
        for h in range(2):
            bank = product(z_first, 0, z2_q, HALF * h, HALF * (h + 1))
            nc.scalar.activation(s_win[0][:, HALF * h : HALF * (h + 1)], bank[:, 0:HALF], ACT.Copy, scale=0.0625)
            nc.scalar.activation(s_copy[0][:, HALF * h : HALF * (h + 1)], bank[:, 0:HALF], ACT.Copy, scale=0.0625)
        for t in range(1, 4):
            bank = product(z_q, t, z2_q)
            nc.scalar.activation(s_copy[t], bank[:], ACT.Copy, scale=0.0625)
            nc.scalar.activation(s_win[t][:, 0:N], bank[:], ACT.Copy, scale=0.0625)
        out_rows = out.rearrange("(p t) v -> p t v", t=4)
        gap = [sb("gap%d" % t, [P, N], F32) for t in range(4)]
        result = [sb("result%d" % t, [P, N], F32) for t in range(4)]
        s6 = [sb("s6_0", [P, N], F32)] + gap[1:]
        nc.vector.tensor_copy(s6[0][:], s_win[0][:].indirect(l_n6[:]))
        for t in range(4):
            nc.vector.tensor_tensor(gap[t][:], s_win[t][:].indirect(l_n5[:]), s_copy[t], ALU.subtract)
        rise = cross
        upper_t = [sb("upper_t%d" % t, [P, N], F32) for t in range(4)]

        def lift(t):
            turned = ps_sum.tile([P, N], F32, name="turned")
            nc.scalar.activation(rise[t][:], gap[t][:], ACT.Relu)
            for a, term in enumerate((s_win[t], rise[t])):
                for c in range(4):
                    cols = slice(P * c, P * (c + 1))
                    turn(turned[:, cols], term[:, cols], a + c == 0, a + c == 4)
            return turned

        def turn_back(t, turned):
            nc.scalar.copy(upper_t[t][:], turned[:])
            back = ps_back.tile([P, N], F32, name="back")
            for c in range(4):
                cols = slice(P * c, P * (c + 1))
                nc.tensor.transpose(back[:, cols], upper_t[t][:, cols], ident[:])
            return back

        lifted = [lift(t) for t in range(3)]
        backs = [turn_back(0, lifted[0])]
        lifted.append(lift(3))
        backs.extend(turn_back(t, lifted[t]) for t in range(1, 4))
        for t in range(1, 4):
            nc.vector.tensor_copy(gap[t][:], s_win[t][:].indirect(l_n6[:]))
        for t in range(4):
            for c0, c1 in ((0, N),) if t < 3 else ((0, HALF), (HALF, N)):
                nc.vector.tensor_tensor(result[t][:, c0:c1], backs[t][:, c0:c1], s6[t][:, c0:c1], ALU.min)
                nc.sync.dma_start(out_rows[:, t, c0:c1], result[t][:, c0:c1])
